import numpy as np, ml_dtypes
CORES = [37,45,53,61,69,109,117,125]
N = 8
import mx_ref
NC, G = 384, 4
C, C2 = np.float32(0.043), np.float32(0.047)
CNT = [[48,48,48,48,48,48,48,48],[48,48,48,48,48,48,48,48],[48,48,48,48,48,48,48,48],[48,48,48,48,48,48,48,48],[48,48,48,48,48,48,48,48],[48,48,48,48,48,48,48,48],[48,48,48,48,48,48,48,48],[48,48,48,48,48,48,48,48]]
OFF = [[sum(c[:e]) for e in range(N + 1)] for c in CNT]
BF = ml_dtypes.bfloat16
def cut(t, i, w=512):
    return t[:, w * i:w * i + w]
def tile(rs):
    return np.stack(rs, axis=2).reshape(128, -1).astype(BF)
def layer(w, X):
    out = []
    for i in range(G):
        for t in range(len(X)):
            p = mx_ref.matmul(mx_ref.quantize(cut(w, len(X) * i + t)), X[t])
            z = p if t == 0 else z + p
        out.append(z)
    return out
def act(Z):
    return [np.maximum(z, 0) * C for z in Z]
def setup_inputs(rng):
    def f(*shape):
        return mx_ref.flush((rng.standard_normal(shape, dtype=np.float32) * np.exp2(rng.integers(-2, 3, shape[:-1] + (1,)))).astype(BF))
    return {"x": f(N, 128, 4 * NC), "w1": f(N, 128, G * 512), "w2": f(N, 128, G * 512), "w3": f(N, 128, 512)}
def setup_inputs_blocks(rng):
    d = setup_inputs(rng)
    for k in ("x", "w3"): d[k] = mx_ref.spread(d[k], rng, 4)
    for k in ("w1", "w2"): d[k] = mx_ref.spread(d[k], rng, 2)
    return d
def setup_inputs_wide(rng):
    d = setup_inputs(rng)
    for k in ("x", "w1", "w2", "w3"): d[k] = mx_ref.flush((d[k].astype(np.float32) * np.exp2(rng.integers(-4, 5, (N, 1, 1))).astype(np.float32)).astype(BF))
    return d
def setup_inputs_zeros(rng):
    d = setup_inputs(rng); v = d["x"].reshape(N, 128, -1, 4).copy()
    v[np.broadcast_to((rng.random((N, 1, v.shape[2], 1)) < 0.33), v.shape)] = 0
    d["x"] = v.reshape(d["x"].shape)
    return d
def act2(Z):
    return [np.maximum(z, 0) * C2 for z in Z]
def reference(x, w1, w2, w3):
    h = [tile(act(layer(w1[j], [mx_ref.quantize(x[j])]))) for j in range(N)]
    g = []
    for e in range(N):
        t = np.concatenate([h[j][:, 4 * OFF[j][e]:4 * OFF[j][e + 1]] for j in range(N)], axis=1)
        g.append(tile(act2(layer(w2[e], [mx_ref.quantize(t)]))))
    y = np.zeros((N, 128, NC), np.float32)
    for j in range(N):
        back = []
        for e in range(N):
            a = sum(CNT[i][e] for i in range(j))
            back.append(g[e][:, 4 * a:4 * a + 4 * CNT[j][e]])
        y[j] = mx_ref.matmul(mx_ref.quantize(w3[j]), mx_ref.quantize(np.concatenate(back, axis=1)))
    return {"y": y}

@@ -1,0 +1,237 @@
+import numpy as np
+from concourse.bass import DstId, RemoteDMATransfer
+from concourse.mybir import dt, AluOpType, ActivationFunctionType
+
+R = 48
+H = 4 * R
+O = 3 * R
+TW = 4 * H
+F8 = "float8_e4m3fn_x4"
+
+SCRATCH = {
+    "x_x": ("sbuf", [128, TW], "bfloat16"), "x_s": ("sbuf", [128, TW], "bfloat16"),
+    "w1b": ("sbuf", [128, 2048], "bfloat16"), "w2b": ("sbuf", [128, 2048], "bfloat16"), "w3b": ("sbuf", [128, 512], "bfloat16"),
+    "h_x": ("sbuf", [128, TW], "bfloat16"), "h_s": ("sbuf", [128, TW], "bfloat16"),
+    "g_x": ("sbuf", [128, TW], "bfloat16"), "g_s": ("sbuf", [128, TW], "bfloat16"),
+    "ybuf": ("sbuf", [128, 384], "float32"),
+}
+for _n, _w in (("xx", H), ("xs", H), ("w1", 512), ("w2", 512), ("w3", 128),
+               ("hx", H), ("bx", H), ("gx", H), ("ax", H),
+               ("hs", O + R + O), ("gs", O + R + O),
+               ("f1", 2 * R), ("f2", 2 * R)):
+    SCRATCH["q" + _n] = ("sbuf", [128, _w], F8)
+    SCRATCH["p" + _n] = ("sbuf", [128, _w], "uint8")
+for _k in range(8):
+    SCRATCH["ps%d" % _k] = ("psum", [128, 512], "float32")
+
+SEMAPHORES = ["ld_x", "ld_s", "ld_w1a", "ld_w1b", "ld_w2", "ld_w3", "q_xx", "q_xs", "q_w2", "q_w3",
+              "a_1x", "a_1s", "a_2x", "a_2s", "q_1x", "q_1s", "q_2x", "q_2s",
+              "b_x", "b_s", "r_x", "r_s", "m_yx", "m_ys", "y_x", "y_s", "st", "sent", "fwd1", "fwd2"]
+SEMAPHORES += ["q_w1%d" % k for k in range(4)]
+SEMAPHORES += ["m_%s%d" % (s, k) for s in ("1x", "1s", "2x", "2s") for k in range(4)]
+
+SIM_CORES = 128
+
+
+def rank_program(g, core, T, topo):
+    cores, n = T.cores, len(T.cores)
+
+    def engines(src, dst):
+        m = topo.mask(src, dst)
+        return [i for i in range(m.bit_length()) if (m >> i) & 1]
+
+    def mk(es):
+        return sum(1 << i for i in es)
+
+    def own_class(j):
+        return [r for r in range(n) if r == j or topo.may_write(cores[j], cores[r])]
+
+    def s_order(j):
+        c = own_class(j)
+        a = c.index(j)
+        return [c[(a + d) % len(c)] for d in range(1, len(c))]
+
+    def x_order(j):
+        c = own_class(j)
+        o = [r for r in range(n) if r not in c]
+        a = c.index(j)
+        return [o[(a + d) % len(o)] for d in range(len(o))]
+
+    def relays(j):
+        me, xo = cores[j], x_order(j)
+        cand = [c for c in range(SIM_CORES) if c != me and topo.chip(c) == topo.chip(me)
+                and all(topo.may_write(c, cores[e]) for e in xo)]
+        near = [c for c in cand if topo.die(c) == topo.die(me)]
+        far = [c for c in cand if topo.die(c) != topo.die(me)]
+        return [(near[0], near[1]), (far[0], far[1])]
+
+    def move(dst, es, rs, q, a, b, to, c, codes):
+        rid, pid = topo.addr(dst)[:2]
+        if codes:
+            s, d = T["q" + q][:, a:b].bitcast(dt.uint8), T["q" + to][:, c:c + b - a].bitcast(dt.uint8)
+        else:
+            s, d = T["p" + q][:, a:b], T["p" + to][:, c:c + b - a]
+        return RemoteDMATransfer(src=s, dst=d, dst_ids=[DstId(rid=rid, pnc=pid)], dma_engine_mask=mk(es), remote_sem=T.sem[rs])
+
+    sent = [0]
+
+    def fused(ts, cnt):
+        g.remote_dma_fused(ts, local_sem=T.sem.sent)
+        sent[0] += cnt
+
+    j = T.rank_of(core)
+    if j is None:
+        for r in range(n):
+            if topo.chip(cores[r]) != topo.chip(core):
+                continue
+            for side, pair in enumerate(relays(r)):
+                if core not in pair:
+                    continue
+                codes = core == pair[0]
+                dests = x_order(r)[2 * side:2 * side + 2]
+                for way, (buf, to, rs) in enumerate((("f1", "bx", "b_x"), ("f2", "ax", "r_x"))):
+                    g.wait_ge(T.sem["fwd%d" % (way + 1)], len(engines(cores[r], core)) // 2)
+                    ts, cnt = [], 0
+                    for i, e in enumerate(dests):
+                        es = engines(core, cores[e])
+                        es = es[:len(es) // 2] if i == 0 else es[len(es) // 2:]
+                        ts.append(move(cores[e], es, rs, buf, i * R, i * R + R, to, x_order(e).index(r) * R, codes))
+                        cnt += len(es)
+                    fused(ts, cnt)
+                g.wait_ge(T.sem.sent, sent[0])
+        return
+
+    xo, so = x_order(j), s_order(j)
+    V, S, E, Y = g.vector, g.scalar, g.tensor, g.sync
+    sem = T.sem
+    c1, c2 = float(np.float32(0.043)), float(np.float32(0.047))
+
+    def off_chip(dst):
+        return engines(core, cores[dst])
+
+    def load_run(q, buf, i, e, s):
+        q.dma_start(T[buf][:, 4 * R * i:4 * R * (i + 1)], T.x[:, 4 * R * e:4 * R * (e + 1)]).then_inc(sem[s], 16)
+
+    for i in (0, 1):
+        load_run(Y, "x_x", i, xo[i], "ld_x")
+        load_run(S, "x_x", i + 2, xo[i + 2], "ld_x")
+    Y.dma_start(T.w1b[:, 0:1024], T.w1[:, 0:1024]).then_inc(sem.ld_w1a, 16)
+    S.dma_start(T.w1b[:, 1024:2048], T.w1[:, 1024:2048]).then_inc(sem.ld_w1b, 16)
+    for i, e in enumerate(so + [j]):
+        load_run(Y, "x_s", i, e, "ld_s")
+    Y.dma_start(T.w2b[:], T.w2[:]).then_inc(sem.ld_w2, 16)
+
+    def quant(q, c, w, src, a, s):
+        V.quantize_mx(T["q" + q][:, c:c + w], T["p" + q][:, c:c + w], T[src][:, a:a + 4 * w]).then_inc(sem[s], 1)
+
+    def products(tag, w, rhs, c, bank, ready=None):
+        for k in range(4):
+            if ready:
+                E.wait_ge(sem[ready % k], 1)
+            E.matmul_mx(T["ps%d" % (bank + k)][:, 0:H], T["q" + w][:, 128 * k:128 * k + 128], T["p" + w][:, 128 * k:128 * k + 128],
+                        T["q" + rhs][:, c:c + H], T["p" + rhs][:, c:c + H], True, True).then_inc(sem["m_%s%d" % (tag, k)], 1)
+
+    def act_s(tag, k, tile, bank, cst):
+        S.wait_ge(sem["m_%s%d" % (tag, k)], 1)
+        S.activation(T[tile][:, k:TW:4], T["ps%d" % (bank + k)][:, 0:H], ActivationFunctionType.Relu, scale=cst).then_inc(sem["a_" + tag], 1)
+
+    def act_v(tag, k, tile, bank, cst):
+        V.wait_ge(sem["m_%s%d" % (tag, k)], 1)
+        V.tensor_scalar(T[tile][:, k:TW:4], T["ps%d" % (bank + k)][:, 0:H], 0.0, cst, AluOpType.max, AluOpType.mult).then_inc(sem["a_" + tag], 1)
+
+    def tile_half(tag, tile, bank, cst, q, c):
+        for k in (0, 2):
+            act_s(tag, k, tile, bank, cst)
+        for k in (1, 3):
+            act_v(tag, k, tile, bank, cst)
+        V.wait_ge(sem["a_" + tag], 4)
+        quant(q, c, H, tile, 0, "q_" + tag)
+
+    def send_x(tag, q, to, rs):
+        g.wait_ge(sem["q_" + tag], 1)
+        for codes in (True, False):
+            ts, cnt = [], 0
+            for side, pair in enumerate(relays(j)):
+                dst = pair[0] if codes else pair[1]
+                es = engines(core, dst)[side::2]
+                ts.append(move(dst, es, rs, q, 2 * R * side, 2 * R * side + 2 * R, to, 0, codes))
+                cnt += len(es)
+            fused(ts, cnt)
+
+    def s_masks(es, codes):
+        k = len(es) // 4
+        return [es[:2 * k], es[2 * k:3 * k], es[3 * k:]] if codes else [es[2 * k:], es[:k], es[k:2 * k]]
+
+    def send_s(tag, q, c, to, c_to, rs):
+        g.wait_ge(sem["q_" + tag], 1)
+        for codes in (True, False):
+            ts, cnt = [], 0
+            for i, e in enumerate(so):
+                es = s_masks(off_chip(e), codes)[i]
+                ts.append(move(cores[e], es, rs, q, c + R * i, c + R * i + R, to, c_to + R * s_order(e).index(j), codes))
+                cnt += len(es)
+            fused(ts, cnt)
+
+    n_off = len(off_chip(so[0]))
+    x_in = len(xo) * n_off
+    s_in = 2 * n_off
+
+    V.wait_ge(sem.ld_x, 64)
+    quant("xx", 0, H, "x_x", 0, "q_xx")
+    V.wait_ge(sem.ld_w1a, 16)
+    for k in range(4):
+        if k == 2:
+            V.wait_ge(sem.ld_w1b, 16)
+        quant("w1", 128 * k, 128, "w1b", 512 * k, "q_w1%d" % k)
+    E.wait_ge(sem.q_xx, 1)
+    products("1x", "w1", "xx", 0, 0, "q_w1%d")
+    tile_half("1x", "h_x", 0, c1, "hx", 0)
+    send_x("1x", "hx", "f1", "fwd1")
+
+    V.wait_ge(sem.ld_s, 64)
+    quant("xs", 0, H, "x_s", 0, "q_xs")
+    E.wait_ge(sem.q_xs, 1)
+    products("1s", "w1", "xs", 0, 4)
+    tile_half("1s", "h_s", 4, c1, "hs", 0)
+    send_s("1s", "hs", 0, "hs", O + R, "b_s")
+
+    V.wait_ge(sem.ld_w2, 16)
+    for k in range(4):
+        quant("w2", 128 * k, 128, "w2b", 512 * k, "q_w2")
+    Y.wait_ge(sem.b_x, x_in)
+    Y.dma_start(T.w3b[:], T.w3[:]).then_inc(sem.ld_w3, 16)
+
+    E.wait_ge(sem.q_w2, 4)
+    E.wait_ge(sem.a_1x, 4)
+    E.wait_ge(sem.b_x, x_in)
+    products("2x", "w2", "bx", 0, 0)
+    tile_half("2x", "g_x", 0, c2, "gx", 0)
+    send_x("2x", "gx", "f2", "fwd2")
+
+    E.wait_ge(sem.a_1s, 4)
+    E.wait_ge(sem.q_1s, 1)
+    E.wait_ge(sem.b_s, s_in)
+    products("2s", "w2", "hs", O, 4)
+    tile_half("2s", "g_s", 4, c2, "gs", O)
+    send_s("2s", "gs", O + R, "gs", 0, "r_s")
+
+    V.wait_ge(sem.ld_w3, 16)
+    quant("w3", 0, 128, "w3b", 0, "q_w3")
+    E.wait_ge(sem.a_2x, 4)
+    E.wait_ge(sem.q_w3, 1)
+    E.wait_ge(sem.q_2s, 1)
+    E.wait_ge(sem.r_s, s_in)
+    E.matmul_mx(T.ps0[:, 0:H], T.qw3[:], T.pw3[:], T.qgs[:, 0:H], T.pgs[:, 0:H], True, True).then_inc(sem.m_ys, 1)
+    E.wait_ge(sem.r_x, x_in)
+    E.matmul_mx(T.ps1[:, 0:H], T.qw3[:], T.pw3[:], T.qax[:], T.pax[:], True, True).then_inc(sem.m_yx, 1)
+    S.wait_ge(sem.m_ys, 1)
+    for i, e in enumerate(so + [j]):
+        S.activation(T.ybuf[:, R * e:R * e + R], T.ps0[:, R * i:R * i + R], ActivationFunctionType.Copy).then_inc(sem.y_s, 1)
+    V.wait_ge(sem.m_yx, 1)
+    for i, e in enumerate(xo):
+        V.tensor_copy(T.ybuf[:, R * e:R * e + R], T.ps1[:, R * i:R * i + R]).then_inc(sem.y_x, 1)
+    Y.wait_ge(sem.y_s, 4)
+    Y.wait_ge(sem.y_x, 4)
+    Y.dma_start(T.y[:], T.ybuf[:]).then_inc(sem.st, 16)
+    Y.wait_ge(sem.st, 16)
+    g.wait_ge(sem.sent, sent[0])

@@ -3,32 +3,38 @@ from concourse.bass import DstId, RemoteDMATransfer
 from concourse.mybir import dt, AluOpType, ActivationFunctionType
 
 R = 48
-H = 4 * R
+P2 = 2 * R
 O = 3 * R
-TW = 4 * H
+H = 4 * R
+W = 128
 F8 = "float8_e4m3fn_x4"
+EARLY, LATE = 0, 1
 
 SCRATCH = {
-    "x_x": ("sbuf", [128, TW], "bfloat16"), "x_s": ("sbuf", [128, TW], "bfloat16"),
+    "x_x": ("sbuf", [128, 4 * H], "bfloat16"), "x_s": ("sbuf", [128, 4 * H], "bfloat16"),
     "w1b": ("sbuf", [128, 2048], "bfloat16"), "w2b": ("sbuf", [128, 2048], "bfloat16"), "w3b": ("sbuf", [128, 512], "bfloat16"),
-    "h_x": ("sbuf", [128, TW], "bfloat16"), "h_s": ("sbuf", [128, TW], "bfloat16"),
-    "g_x": ("sbuf", [128, TW], "bfloat16"), "g_s": ("sbuf", [128, TW], "bfloat16"),
+    "h_x": ("sbuf", [128, 4 * H], "bfloat16"), "h_s": ("sbuf", [128, 4 * H], "bfloat16"),
+    "g_t": ("sbuf", [128, 8 * H], "bfloat16"),
     "ybuf": ("sbuf", [128, 384], "float32"),
 }
 for _n, _w in (("xx", H), ("xs", H), ("w1", 512), ("w2", 512), ("w3", 128),
-               ("hx", H), ("bx", H), ("gx", H), ("ax", H),
-               ("hs", O + R + O), ("gs", O + R + O),
-               ("f1", 2 * R), ("f2", 2 * R)):
+               ("h1", W), ("h2", W),
+               ("hs", 2 * O + R + H),
+               ("g1", H + R + P2),
+               ("g2", W), ("g3", O),
+               ("as", O),
+               ("f1", P2), ("f2", P2)):
     SCRATCH["q" + _n] = ("sbuf", [128, _w], F8)
     SCRATCH["p" + _n] = ("sbuf", [128, _w], "uint8")
 for _k in range(8):
     SCRATCH["ps%d" % _k] = ("psum", [128, 512], "float32")
 
 SEMAPHORES = ["ld_x", "ld_s", "ld_w1a", "ld_w1b", "ld_w2", "ld_w3", "q_xx", "q_xs", "q_w2", "q_w3",
-              "a_1x", "a_1s", "a_2x", "a_2s", "q_1x", "q_1s", "q_2x", "q_2s",
-              "b_x", "b_s", "r_x", "r_s", "m_yx", "m_ys", "y_x", "y_s", "st", "sent", "fwd1", "fwd2"]
+              "a_1x", "a_1y", "a_1z", "a_1s", "a_2a", "a_2b", "a_2s", "q_1a", "q_1b", "q_1s", "q_2a", "q_2b", "q_2s",
+              "b_0", "b_1", "b_s0", "b_s", "r_0", "r_1", "r_s", "m_yo", "m_ya", "m_yb", "m_ys", "y_v", "y_s", "st",
+              "sent", "fwd1", "fwd2"]
 SEMAPHORES += ["q_w1%d" % k for k in range(4)]
-SEMAPHORES += ["m_%s%d" % (s, k) for s in ("1x", "1s", "2x", "2s") for k in range(4)]
+SEMAPHORES += ["m_%s%d" % (s, k) for s in ("1x", "1s", "2a", "2b", "2s") for k in range(4)]
 
 SIM_CORES = 128
 
@@ -51,19 +57,33 @@ def rank_program(g, core, T, topo):
         a = c.index(j)
         return [c[(a + d) % len(c)] for d in range(1, len(c))]
 
-    def x_order(j):
+    def si_order(j):
+        return sorted((r for r in own_class(j) if r != j), key=lambda r: s_order(r).index(j))
+
+    def out_order(j):
         c = own_class(j)
         o = [r for r in range(n) if r not in c]
         a = c.index(j)
         return [o[(a + d) % len(o)] for d in range(len(o))]
 
+    def in_order(j):
+        o = out_order(j)
+        return [r for r in o if j in out_order(r)[:2]] + [r for r in o if j in out_order(r)[2:]]
+
     def relays(j):
-        me, xo = cores[j], x_order(j)
+        me, xo = cores[j], out_order(j)
         cand = [c for c in range(SIM_CORES) if c != me and topo.chip(c) == topo.chip(me)
                 and all(topo.may_write(c, cores[e]) for e in xo)]
         near = [c for c in cand if topo.die(c) == topo.die(me)]
         far = [c for c in cand if topo.die(c) != topo.die(me)]
         return [(near[0], near[1]), (far[0], far[1])]
+
+    def b_col(e, r):
+        return 2 * O + R + R * in_order(e).index(r)
+
+    def a_col(j, r):
+        i = out_order(j).index(r)
+        return P2 + R * i if i < 2 else R * (i - 2)
 
     def move(dst, es, rs, q, a, b, to, c, codes):
         rid, pid = topo.addr(dst)[:2]
@@ -88,20 +108,21 @@ def rank_program(g, core, T, topo):
                 if core not in pair:
                     continue
                 codes = core == pair[0]
-                dests = x_order(r)[2 * side:2 * side + 2]
-                for way, (buf, to, rs) in enumerate((("f1", "bx", "b_x"), ("f2", "ax", "r_x"))):
-                    g.wait_ge(T.sem["fwd%d" % (way + 1)], len(engines(cores[r], core)) // 2)
+                for way, (buf, to, rs) in enumerate((("f1", "hs", "b_%d"), ("f2", "g1", "r_%d"))):
+                    dests = (in_order(r) if way else out_order(r))[2 * side:2 * side + 2]
+                    g.wait_ge(T.sem["fwd%d" % (way + 1)], len(engines(cores[r], core)))
                     ts, cnt = [], 0
                     for i, e in enumerate(dests):
                         es = engines(core, cores[e])
                         es = es[:len(es) // 2] if i == 0 else es[len(es) // 2:]
-                        ts.append(move(cores[e], es, rs, buf, i * R, i * R + R, to, x_order(e).index(r) * R, codes))
+                        c = a_col(e, r) if way else b_col(e, r)
+                        ts.append(move(cores[e], es, rs % side, buf, i * R, i * R + R, to, c, codes))
                         cnt += len(es)
                     fused(ts, cnt)
                 g.wait_ge(T.sem.sent, sent[0])
         return
 
-    xo, so = x_order(j), s_order(j)
+    xo, so, si = out_order(j), s_order(j), si_order(j)
     V, S, E, Y = g.vector, g.scalar, g.tensor, g.sync
     sem = T.sem
     c1, c2 = float(np.float32(0.043)), float(np.float32(0.047))
@@ -115,123 +136,163 @@ def rank_program(g, core, T, topo):
     for i in (0, 1):
         load_run(Y, "x_x", i, xo[i], "ld_x")
         load_run(S, "x_x", i + 2, xo[i + 2], "ld_x")
-    Y.dma_start(T.w1b[:, 0:1024], T.w1[:, 0:1024]).then_inc(sem.ld_w1a, 16)
-    S.dma_start(T.w1b[:, 1024:2048], T.w1[:, 1024:2048]).then_inc(sem.ld_w1b, 16)
+    Y.dma_start(T.w1b[:, 0:1536], T.w1[:, 0:1536]).then_inc(sem.ld_w1a, 16)
+    Y.dma_start(T.w1b[:, 1536:2048], T.w1[:, 1536:2048]).then_inc(sem.ld_w1b, 16)
     for i, e in enumerate(so + [j]):
         load_run(Y, "x_s", i, e, "ld_s")
     Y.dma_start(T.w2b[:], T.w2[:]).then_inc(sem.ld_w2, 16)
 
     def quant(q, c, w, src, a, s):
-        V.quantize_mx(T["q" + q][:, c:c + w], T["p" + q][:, c:c + w], T[src][:, a:a + 4 * w]).then_inc(sem[s], 1)
+        V.quantize_mx(T["q" + q][:, c:c + w], T["p" + q][:, c:c + w], T[src][:, 4 * a:4 * (a + w)]).then_inc(sem[s], 1)
 
-    def products(tag, w, rhs, c, bank, ready=None):
+    def products(tag, w, rhs, c, width, bank, ready=None):
         for k in range(4):
             if ready:
                 E.wait_ge(sem[ready % k], 1)
-            E.matmul_mx(T["ps%d" % (bank + k)][:, 0:H], T["q" + w][:, 128 * k:128 * k + 128], T["p" + w][:, 128 * k:128 * k + 128],
-                        T["q" + rhs][:, c:c + H], T["p" + rhs][:, c:c + H], True, True).then_inc(sem["m_%s%d" % (tag, k)], 1)
+            E.matmul_mx(T["ps%d" % (bank + k)][:, 0:width], T["q" + w][:, 128 * k:128 * k + 128], T["p" + w][:, 128 * k:128 * k + 128],
+                        T["q" + rhs][:, c:c + width], T["p" + rhs][:, c:c + width], True, True).then_inc(sem["m_%s%d" % (tag, k)], 1)
 
-    def act_s(tag, k, tile, bank, cst):
+    def act_s(tag, k, tile, c, width, bank, f, cst, done):
         S.wait_ge(sem["m_%s%d" % (tag, k)], 1)
-        S.activation(T[tile][:, k:TW:4], T["ps%d" % (bank + k)][:, 0:H], ActivationFunctionType.Relu, scale=cst).then_inc(sem["a_" + tag], 1)
+        S.activation(T[tile][:, 4 * c + k:4 * (c + width):4], T["ps%d" % (bank + k)][:, f:f + width],
+                     ActivationFunctionType.Relu, scale=cst).then_inc(sem[done], 1)
 
-    def act_v(tag, k, tile, bank, cst):
+    def act_v(tag, k, tile, c, width, bank, f, cst, done):
         V.wait_ge(sem["m_%s%d" % (tag, k)], 1)
-        V.tensor_scalar(T[tile][:, k:TW:4], T["ps%d" % (bank + k)][:, 0:H], 0.0, cst, AluOpType.max, AluOpType.mult).then_inc(sem["a_" + tag], 1)
+        V.tensor_scalar(T[tile][:, 4 * c + k:4 * (c + width):4], T["ps%d" % (bank + k)][:, f:f + width], 0.0, cst,
+                        AluOpType.max, AluOpType.mult).then_inc(sem[done], 1)
 
-    def tile_half(tag, tile, bank, cst, q, c):
+    def make_tile(tag, tile, c, width, bank, f, cst):
         for k in (0, 2):
-            act_s(tag, k, tile, bank, cst)
+            act_s(tag, k, tile, c, width, bank, f, cst, "a_" + tag)
         for k in (1, 3):
-            act_v(tag, k, tile, bank, cst)
+            act_v(tag, k, tile, c, width, bank, f, cst, "a_" + tag)
         V.wait_ge(sem["a_" + tag], 4)
-        quant(q, c, H, tile, 0, "q_" + tag)
 
-    def send_x(tag, q, to, rs):
-        g.wait_ge(sem["q_" + tag], 1)
+    def send_x(side, ready, q, a, to, rs):
+        g.wait_ge(sem[ready], 1)
+        for codes, dst in zip((True, False), relays(j)[side]):
+            es = engines(core, dst)
+            fused([move(dst, es, rs, q, a, a + P2, to, 0, codes)], len(es))
+
+    def send_s(ready, q, a, dests, to, col, rs):
+        g.wait_ge(sem[ready], 1)
         for codes in (True, False):
             ts, cnt = [], 0
-            for side, pair in enumerate(relays(j)):
-                dst = pair[0] if codes else pair[1]
-                es = engines(core, dst)[side::2]
-                ts.append(move(dst, es, rs, q, 2 * R * side, 2 * R * side + 2 * R, to, 0, codes))
-                cnt += len(es)
+            for i, e in enumerate(dests):
+                es = off_chip(e)
+                k = len(es) // len(dests)
+                ts.append(move(cores[e], es[k * i:k * i + k], rs, q, a + R * i, a + R * i + R, to, col(e), codes))
+                cnt += k
             fused(ts, cnt)
 
-    def s_masks(es, codes):
-        k = len(es) // 4
-        return [es[:2 * k], es[2 * k:3 * k], es[3 * k:]] if codes else [es[2 * k:], es[:k], es[k:2 * k]]
+    def s_in_col(e):
+        i = si_order(e).index(j)
+        return O + R + (R * (i - 1) if i else P2)
 
-    def send_s(tag, q, c, to, c_to, rs):
-        g.wait_ge(sem["q_" + tag], 1)
-        for codes in (True, False):
-            ts, cnt = [], 0
-            for i, e in enumerate(so):
-                es = s_masks(off_chip(e), codes)[i]
-                ts.append(move(cores[e], es, rs, q, c + R * i, c + R * i + R, to, c_to + R * s_order(e).index(j), codes))
-                cnt += len(es)
-            fused(ts, cnt)
+    def s_home_col(e):
+        return R * s_order(e).index(j)
 
     n_off = len(off_chip(so[0]))
-    x_in = len(xo) * n_off
+    x_in = 2 * n_off
     s_in = 2 * n_off
 
     V.wait_ge(sem.ld_x, 64)
     quant("xx", 0, H, "x_x", 0, "q_xx")
     V.wait_ge(sem.ld_w1a, 16)
     for k in range(4):
-        if k == 2:
+        if k == 3:
             V.wait_ge(sem.ld_w1b, 16)
-        quant("w1", 128 * k, 128, "w1b", 512 * k, "q_w1%d" % k)
+        quant("w1", 128 * k, 128, "w1b", 128 * k, "q_w1%d" % k)
     E.wait_ge(sem.q_xx, 1)
-    products("1x", "w1", "xx", 0, 0, "q_w1%d")
-    tile_half("1x", "h_x", 0, c1, "hx", 0)
-    send_x("1x", "hx", "f1", "fwd1")
+    products("1x", "w1", "xx", 0, H, 0, "q_w1%d")
+    for k in range(3):
+        act_s("1x", k, "h_x", 0, H, 0, 0, c1, "a_1x")
+    act_v("1x", 3, "h_x", 0, W, 0, 0, c1, "a_1y")
+    S.wait_ge(sem.a_1y, 1)
+    act_s("1x", 3, "h_x", W, H - W, 0, W, c1, "a_1z")
+    V.wait_ge(sem.a_1x, 3)
+    V.wait_ge(sem.a_1y, 1)
+    quant("h1", 0, W, "h_x", 0, "q_1a")
+    V.wait_ge(sem.a_1z, 1)
+    quant("h2", 0, W, "h_x", H - W, "q_1b")
+    send_x(EARLY, "q_1a", "h1", 0, "f1", "fwd1")
+    send_x(LATE, "q_1b", "h2", W - P2, "f1", "fwd1")
 
     V.wait_ge(sem.ld_s, 64)
     quant("xs", 0, H, "x_s", 0, "q_xs")
     E.wait_ge(sem.q_xs, 1)
-    products("1s", "w1", "xs", 0, 4)
-    tile_half("1s", "h_s", 4, c1, "hs", 0)
-    send_s("1s", "hs", 0, "hs", O + R, "b_s")
+    products("1s", "w1", "xs", 0, H, 4)
+    make_tile("1s", "h_s", 0, H, 4, 0, c1)
+    quant("hs", 0, H, "h_s", 0, "q_1s")
+    send_s("q_1s", "hs", 0, so[:1], "hs", s_in_col, "b_s0")
+    send_s("q_1s", "hs", R, so[1:], "hs", s_in_col, "b_s")
 
     V.wait_ge(sem.ld_w2, 16)
     for k in range(4):
-        quant("w2", 128 * k, 128, "w2b", 512 * k, "q_w2")
-    Y.wait_ge(sem.b_x, x_in)
+        quant("w2", 128 * k, 128, "w2b", 128 * k, "q_w2")
+    Y.wait_ge(sem.b_0, x_in)
     Y.dma_start(T.w3b[:], T.w3[:]).then_inc(sem.ld_w3, 16)
 
     E.wait_ge(sem.q_w2, 4)
-    E.wait_ge(sem.a_1x, 4)
-    E.wait_ge(sem.b_x, x_in)
-    products("2x", "w2", "bx", 0, 0)
-    tile_half("2x", "g_x", 0, c2, "gx", 0)
-    send_x("2x", "gx", "f2", "fwd2")
+    E.wait_ge(sem.a_1x, 3)
+    E.wait_ge(sem.a_1z, 1)
+    E.wait_ge(sem.b_s0, s_in)
+    E.wait_ge(sem.b_0, x_in)
+    products("2a", "w2", "hs", 2 * O, O, 0)
+    make_tile("2a", "g_t", 0, O, 0, 0, c2)
+    quant("g1", H, O, "g_t", 0, "q_2a")
+    send_x(EARLY, "q_2a", "g1", H + R, "f2", "fwd2")
 
     E.wait_ge(sem.a_1s, 4)
+    E.wait_ge(sem.b_1, x_in)
+    products("2b", "w2", "hs", 3 * O + P2 - W, W, 4)
+    make_tile("2b", "g_t", O, P2, 4, W - P2, c2)
+    quant("g2", 0, W, "g_t", O + P2 - W, "q_2b")
+    send_x(LATE, "q_2b", "g2", W - P2, "f2", "fwd2")
+    send_s("q_2a", "g1", H, si[:1], "as", s_home_col, "r_s")
+
+    E.wait_ge(sem.a_2a, 4)
     E.wait_ge(sem.q_1s, 1)
     E.wait_ge(sem.b_s, s_in)
-    products("2s", "w2", "hs", O, 4)
-    tile_half("2s", "g_s", 4, c2, "gs", O)
-    send_s("2s", "gs", O + R, "gs", 0, "r_s")
+    products("2s", "w2", "hs", O, O, 0)
+    make_tile("2s", "g_t", O + P2, O, 0, 0, c2)
+    quant("g3", 0, O, "g_t", O + P2, "q_2s")
+    send_s("q_2s", "g3", R, si[1:], "as", s_home_col, "r_s")
 
     V.wait_ge(sem.ld_w3, 16)
     quant("w3", 0, 128, "w3b", 0, "q_w3")
-    E.wait_ge(sem.a_2x, 4)
+
+    def last(bank, rhs, c, width, done):
+        E.matmul_mx(T["ps%d" % bank][:, 0:width], T.qw3[:], T.pw3[:], T["q" + rhs][:, c:c + width], T["p" + rhs][:, c:c + width],
+                    True, True).then_inc(sem[done], 1)
+
     E.wait_ge(sem.q_w3, 1)
+    E.wait_ge(sem.a_2b, 4)
+    E.wait_ge(sem.q_2a, 1)
     E.wait_ge(sem.q_2s, 1)
-    E.wait_ge(sem.r_s, s_in)
-    E.matmul_mx(T.ps0[:, 0:H], T.qw3[:], T.pw3[:], T.qgs[:, 0:H], T.pgs[:, 0:H], True, True).then_inc(sem.m_ys, 1)
-    E.wait_ge(sem.r_x, x_in)
-    E.matmul_mx(T.ps1[:, 0:H], T.qw3[:], T.pw3[:], T.qax[:], T.pax[:], True, True).then_inc(sem.m_yx, 1)
+    last(4, "g3", 0, W, "m_yo")
+    E.wait_ge(sem.r_0, x_in)
+    last(5, "g1", P2, W, "m_ya")
+    E.wait_ge(sem.r_s, 2 * s_in)
+    last(6, "as", 0, O, "m_ys")
+    E.wait_ge(sem.r_1, x_in)
+    last(7, "g1", 0, W, "m_yb")
+
+    def home(call, bank, runs, done):
+        for i, e in enumerate(runs):
+            call(T.ybuf[:, R * e:R * e + R], T["ps%d" % bank][:, R * i:R * i + R]).then_inc(sem[done], 1)
+
+    V.wait_ge(sem.m_yo, 1)
+    home(V.tensor_copy, 4, [j], "y_v")
+    V.wait_ge(sem.m_ya, 1)
+    home(V.tensor_copy, 5, xo[:2], "y_v")
     S.wait_ge(sem.m_ys, 1)
-    for i, e in enumerate(so + [j]):
-        S.activation(T.ybuf[:, R * e:R * e + R], T.ps0[:, R * i:R * i + R], ActivationFunctionType.Copy).then_inc(sem.y_s, 1)
-    V.wait_ge(sem.m_yx, 1)
-    for i, e in enumerate(xo):
-        V.tensor_copy(T.ybuf[:, R * e:R * e + R], T.ps1[:, R * i:R * i + R]).then_inc(sem.y_x, 1)
-    Y.wait_ge(sem.y_s, 4)
-    Y.wait_ge(sem.y_x, 4)
+    home(lambda out, in_: S.activation(out, in_, ActivationFunctionType.Copy), 6, so, "y_s")
+    V.wait_ge(sem.m_yb, 1)
+    home(V.tensor_copy, 7, xo[2:], "y_v")
+    Y.wait_ge(sem.y_s, len(so))
+    Y.wait_ge(sem.y_v, len(xo) + 1)
     Y.dma_start(T.y[:], T.ybuf[:]).then_inc(sem.st, 16)
     Y.wait_ge(sem.st, 16)
     g.wait_ge(sem.sent, sent[0])

import numpy as np
from concourse.bass import DstId, RemoteDMATransfer
from concourse.mybir import dt, AluOpType, ActivationFunctionType

R = 48
P2 = 2 * R
O = 3 * R
H = 4 * R
W = 128
F8 = "float8_e4m3fn_x4"
EARLY, LATE = 0, 1

SCRATCH = {
    "x_x": ("sbuf", [128, 4 * H], "bfloat16"), "x_s": ("sbuf", [128, 4 * H], "bfloat16"),
    "w1b": ("sbuf", [128, 2048], "bfloat16"), "w2b": ("sbuf", [128, 2048], "bfloat16"), "w3b": ("sbuf", [128, 512], "bfloat16"),
    "h_x": ("sbuf", [128, 4 * H], "bfloat16"), "h_s": ("sbuf", [128, 4 * H], "bfloat16"),
    "g_t": ("sbuf", [128, 8 * H], "bfloat16"),
    "ybuf": ("sbuf", [128, 384], "float32"),
}
for _n, _w in (("xx", H), ("xs", H), ("w1", 512), ("w2", 512), ("w3", 128),
               ("h1", W), ("h2", W),
               ("hs", 2 * O + R + H),
               ("g1", H + R + P2),
               ("g2", W), ("g3", O),
               ("as", O),
               ("f1", P2), ("f2", P2)):
    SCRATCH["q" + _n] = ("sbuf", [128, _w], F8)
    SCRATCH["p" + _n] = ("sbuf", [128, _w], "uint8")
for _k in range(8):
    SCRATCH["ps%d" % _k] = ("psum", [128, 512], "float32")

SEMAPHORES = ["ld_x", "ld_s", "ld_w1a", "ld_w1b", "ld_w2", "ld_w3", "q_xx", "q_xs", "q_w2", "q_w3",
              "a_1x", "a_1y", "a_1z", "a_1s", "a_2a", "a_2b", "a_2s", "q_1a", "q_1b", "q_1s", "q_2a", "q_2b", "q_2s",
              "b_0", "b_1", "b_s0", "b_s", "r_0", "r_1", "r_s", "m_yo", "m_ya", "m_yb", "m_ys", "y_v", "y_s", "st",
              "sent", "fwd1", "fwd2"]
SEMAPHORES += ["q_w1%d" % k for k in range(4)]
SEMAPHORES += ["m_%s%d" % (s, k) for s in ("1x", "1s", "2a", "2b", "2s") for k in range(4)]

SIM_CORES = 128


def rank_program(g, core, T, topo):
    cores, n = T.cores, len(T.cores)

    def engines(src, dst):
        m = topo.mask(src, dst)
        return [i for i in range(m.bit_length()) if (m >> i) & 1]

    def mk(es):
        return sum(1 << i for i in es)

    def own_class(j):
        return [r for r in range(n) if r == j or topo.may_write(cores[j], cores[r])]

    def s_order(j):
        c = own_class(j)
        a = c.index(j)
        return [c[(a + d) % len(c)] for d in range(1, len(c))]

    def si_order(j):
        return sorted((r for r in own_class(j) if r != j), key=lambda r: s_order(r).index(j))

    def out_order(j):
        c = own_class(j)
        o = [r for r in range(n) if r not in c]
        a = c.index(j)
        return [o[(a + d) % len(o)] for d in range(len(o))]

    def in_order(j):
        o = out_order(j)
        return [r for r in o if j in out_order(r)[:2]] + [r for r in o if j in out_order(r)[2:]]

    def relays(j):
        me, xo = cores[j], out_order(j)
        cand = [c for c in range(SIM_CORES) if c != me and topo.chip(c) == topo.chip(me)
                and all(topo.may_write(c, cores[e]) for e in xo)]
        near = [c for c in cand if topo.die(c) == topo.die(me)]
        far = [c for c in cand if topo.die(c) != topo.die(me)]
        return [(near[0], near[1]), (far[0], far[1])]

    def b_col(e, r):
        return 2 * O + R + R * in_order(e).index(r)

    def a_col(j, r):
        i = out_order(j).index(r)
        return P2 + R * i if i < 2 else R * (i - 2)

    def move(dst, es, rs, q, a, b, to, c, codes):
        rid, pid = topo.addr(dst)[:2]
        if codes:
            s, d = T["q" + q][:, a:b].bitcast(dt.uint8), T["q" + to][:, c:c + b - a].bitcast(dt.uint8)
        else:
            s, d = T["p" + q][:, a:b], T["p" + to][:, c:c + b - a]
        return RemoteDMATransfer(src=s, dst=d, dst_ids=[DstId(rid=rid, pnc=pid)], dma_engine_mask=mk(es), remote_sem=T.sem[rs])

    sent = [0]

    def fused(ts, cnt):
        g.remote_dma_fused(ts, local_sem=T.sem.sent)
        sent[0] += cnt

    j = T.rank_of(core)
    if j is None:
        for r in range(n):
            if topo.chip(cores[r]) != topo.chip(core):
                continue
            for side, pair in enumerate(relays(r)):
                if core not in pair:
                    continue
                codes = core == pair[0]
                for way, (buf, to, rs) in enumerate((("f1", "hs", "b_%d"), ("f2", "g1", "r_%d"))):
                    dests = (in_order(r) if way else out_order(r))[2 * side:2 * side + 2]
                    g.wait_ge(T.sem["fwd%d" % (way + 1)], len(engines(cores[r], core)))
                    ts, cnt = [], 0
                    for i, e in enumerate(dests):
                        es = engines(core, cores[e])
                        es = es[:len(es) // 2] if i == 0 else es[len(es) // 2:]
                        c = a_col(e, r) if way else b_col(e, r)
                        ts.append(move(cores[e], es, rs % side, buf, i * R, i * R + R, to, c, codes))
                        cnt += len(es)
                    fused(ts, cnt)
                g.wait_ge(T.sem.sent, sent[0])
        return

    xo, so, si = out_order(j), s_order(j), si_order(j)
    V, S, E, Y = g.vector, g.scalar, g.tensor, g.sync
    sem = T.sem
    c1, c2 = float(np.float32(0.043)), float(np.float32(0.047))

    def off_chip(dst):
        return engines(core, cores[dst])

    def load_run(q, buf, i, e, s):
        q.dma_start(T[buf][:, 4 * R * i:4 * R * (i + 1)], T.x[:, 4 * R * e:4 * R * (e + 1)]).then_inc(sem[s], 16)

    for i in (0, 1):
        load_run(Y, "x_x", i, xo[i], "ld_x")
        load_run(S, "x_x", i + 2, xo[i + 2], "ld_x")
    Y.dma_start(T.w1b[:, 0:1536], T.w1[:, 0:1536]).then_inc(sem.ld_w1a, 16)
    Y.dma_start(T.w1b[:, 1536:2048], T.w1[:, 1536:2048]).then_inc(sem.ld_w1b, 16)
    for i, e in enumerate(so + [j]):
        load_run(Y, "x_s", i, e, "ld_s")
    Y.dma_start(T.w2b[:], T.w2[:]).then_inc(sem.ld_w2, 16)

    def quant(q, c, w, src, a, s):
        V.quantize_mx(T["q" + q][:, c:c + w], T["p" + q][:, c:c + w], T[src][:, 4 * a:4 * (a + w)]).then_inc(sem[s], 1)

    def products(tag, w, rhs, c, width, bank, ready=None):
        for k in range(4):
            if ready:
                E.wait_ge(sem[ready % k], 1)
            E.matmul_mx(T["ps%d" % (bank + k)][:, 0:width], T["q" + w][:, 128 * k:128 * k + 128], T["p" + w][:, 128 * k:128 * k + 128],
                        T["q" + rhs][:, c:c + width], T["p" + rhs][:, c:c + width], True, True).then_inc(sem["m_%s%d" % (tag, k)], 1)

    def act_s(tag, k, tile, c, width, bank, f, cst, done):
        S.wait_ge(sem["m_%s%d" % (tag, k)], 1)
        S.activation(T[tile][:, 4 * c + k:4 * (c + width):4], T["ps%d" % (bank + k)][:, f:f + width],
                     ActivationFunctionType.Relu, scale=cst).then_inc(sem[done], 1)

    def act_v(tag, k, tile, c, width, bank, f, cst, done):
        V.wait_ge(sem["m_%s%d" % (tag, k)], 1)
        V.tensor_scalar(T[tile][:, 4 * c + k:4 * (c + width):4], T["ps%d" % (bank + k)][:, f:f + width], 0.0, cst,
                        AluOpType.max, AluOpType.mult).then_inc(sem[done], 1)

    def make_tile(tag, tile, c, width, bank, f, cst):
        for k in (0, 2):
            act_s(tag, k, tile, c, width, bank, f, cst, "a_" + tag)
        for k in (1, 3):
            act_v(tag, k, tile, c, width, bank, f, cst, "a_" + tag)
        V.wait_ge(sem["a_" + tag], 4)

    def send_x(side, ready, q, a, to, rs):
        g.wait_ge(sem[ready], 1)
        for codes, dst in zip((True, False), relays(j)[side]):
            es = engines(core, dst)
            fused([move(dst, es, rs, q, a, a + P2, to, 0, codes)], len(es))

    def send_s(ready, q, a, dests, to, col, rs):
        g.wait_ge(sem[ready], 1)
        for codes in (True, False):
            ts, cnt = [], 0
            for i, e in enumerate(dests):
                es = off_chip(e)
                k = len(es) // len(dests)
                ts.append(move(cores[e], es[k * i:k * i + k], rs, q, a + R * i, a + R * i + R, to, col(e), codes))
                cnt += k
            fused(ts, cnt)

    def s_in_col(e):
        i = si_order(e).index(j)
        return O + R + (R * (i - 1) if i else P2)

    def s_home_col(e):
        return R * s_order(e).index(j)

    n_off = len(off_chip(so[0]))
    x_in = 2 * n_off
    s_in = 2 * n_off

    V.wait_ge(sem.ld_x, 64)
    quant("xx", 0, H, "x_x", 0, "q_xx")
    V.wait_ge(sem.ld_w1a, 16)
    for k in range(4):
        if k == 3:
            V.wait_ge(sem.ld_w1b, 16)
        quant("w1", 128 * k, 128, "w1b", 128 * k, "q_w1%d" % k)
    E.wait_ge(sem.q_xx, 1)
    products("1x", "w1", "xx", 0, H, 0, "q_w1%d")
    for k in range(3):
        act_s("1x", k, "h_x", 0, H, 0, 0, c1, "a_1x")
    act_v("1x", 3, "h_x", 0, W, 0, 0, c1, "a_1y")
    S.wait_ge(sem.a_1y, 1)
    act_s("1x", 3, "h_x", W, H - W, 0, W, c1, "a_1z")
    V.wait_ge(sem.a_1x, 3)
    V.wait_ge(sem.a_1y, 1)
    quant("h1", 0, W, "h_x", 0, "q_1a")
    V.wait_ge(sem.a_1z, 1)
    quant("h2", 0, W, "h_x", H - W, "q_1b")
    send_x(EARLY, "q_1a", "h1", 0, "f1", "fwd1")
    send_x(LATE, "q_1b", "h2", W - P2, "f1", "fwd1")

    V.wait_ge(sem.ld_s, 64)
    quant("xs", 0, H, "x_s", 0, "q_xs")
    E.wait_ge(sem.q_xs, 1)
    products("1s", "w1", "xs", 0, H, 4)
    make_tile("1s", "h_s", 0, H, 4, 0, c1)
    quant("hs", 0, H, "h_s", 0, "q_1s")
    send_s("q_1s", "hs", 0, so[:1], "hs", s_in_col, "b_s0")
    send_s("q_1s", "hs", R, so[1:], "hs", s_in_col, "b_s")

    V.wait_ge(sem.ld_w2, 16)
    for k in range(4):
        quant("w2", 128 * k, 128, "w2b", 128 * k, "q_w2")
    Y.wait_ge(sem.b_0, x_in)
    Y.dma_start(T.w3b[:], T.w3[:]).then_inc(sem.ld_w3, 16)

    E.wait_ge(sem.q_w2, 4)
    E.wait_ge(sem.a_1x, 3)
    E.wait_ge(sem.a_1z, 1)
    E.wait_ge(sem.b_s0, s_in)
    E.wait_ge(sem.b_0, x_in)
    products("2a", "w2", "hs", 2 * O, O, 0)
    make_tile("2a", "g_t", 0, O, 0, 0, c2)
    quant("g1", H, O, "g_t", 0, "q_2a")
    send_x(EARLY, "q_2a", "g1", H + R, "f2", "fwd2")

    E.wait_ge(sem.a_1s, 4)
    E.wait_ge(sem.b_1, x_in)
    products("2b", "w2", "hs", 3 * O + P2 - W, W, 4)
    make_tile("2b", "g_t", O, P2, 4, W - P2, c2)
    quant("g2", 0, W, "g_t", O + P2 - W, "q_2b")
    send_x(LATE, "q_2b", "g2", W - P2, "f2", "fwd2")
    send_s("q_2a", "g1", H, si[:1], "as", s_home_col, "r_s")

    E.wait_ge(sem.a_2a, 4)
    E.wait_ge(sem.q_1s, 1)
    E.wait_ge(sem.b_s, s_in)
    products("2s", "w2", "hs", O, O, 0)
    make_tile("2s", "g_t", O + P2, O, 0, 0, c2)
    quant("g3", 0, O, "g_t", O + P2, "q_2s")
    send_s("q_2s", "g3", R, si[1:], "as", s_home_col, "r_s")

    V.wait_ge(sem.ld_w3, 16)
    quant("w3", 0, 128, "w3b", 0, "q_w3")

    def last(bank, rhs, c, width, done):
        E.matmul_mx(T["ps%d" % bank][:, 0:width], T.qw3[:], T.pw3[:], T["q" + rhs][:, c:c + width], T["p" + rhs][:, c:c + width],
                    True, True).then_inc(sem[done], 1)

    E.wait_ge(sem.q_w3, 1)
    E.wait_ge(sem.a_2b, 4)
    E.wait_ge(sem.q_2a, 1)
    E.wait_ge(sem.q_2s, 1)
    last(4, "g3", 0, W, "m_yo")
    E.wait_ge(sem.r_0, x_in)
    last(5, "g1", P2, W, "m_ya")
    E.wait_ge(sem.r_s, 2 * s_in)
    last(6, "as", 0, O, "m_ys")
    E.wait_ge(sem.r_1, x_in)
    last(7, "g1", 0, W, "m_yb")

    def home(call, bank, runs, done):
        for i, e in enumerate(runs):
            call(T.ybuf[:, R * e:R * e + R], T["ps%d" % bank][:, R * i:R * i + R]).then_inc(sem[done], 1)

    V.wait_ge(sem.m_yo, 1)
    home(V.tensor_copy, 4, [j], "y_v")
    V.wait_ge(sem.m_ya, 1)
    home(V.tensor_copy, 5, xo[:2], "y_v")
    S.wait_ge(sem.m_ys, 1)
    home(lambda out, in_: S.activation(out, in_, ActivationFunctionType.Copy), 6, so, "y_s")
    V.wait_ge(sem.m_yb, 1)
    home(V.tensor_copy, 7, xo[2:], "y_v")
    Y.wait_ge(sem.y_s, len(so))
    Y.wait_ge(sem.y_v, len(xo) + 1)
    Y.dma_start(T.y[:], T.ybuf[:]).then_inc(sem.st, 16)
    Y.wait_ge(sem.st, 16)
    g.wait_ge(sem.sent, sent[0])
